import numpy as np, ml_dtypes
CORES = [21,85,149,213,277,341,405,469]
N = 8
import mx_ref
NC, KT, G, WT = 128, 1, 2, 1
C = np.float32(0.041)
BF = ml_dtypes.bfloat16
def cut(t, i, w=512):
    return t[:, w * i:w * i + w]
def tile(rs):
    return np.stack(rs, axis=2).reshape(128, -1).astype(BF)
def layer(w, X):
    out = []
    for i in range(G):
        for t in range(len(X)):
            p = mx_ref.matmul(mx_ref.quantize(cut(w, len(X) * i + t)), X[t])
            z = p if t == 0 else z + p
        out.append(z)
    return out
def act(Z):
    return [np.maximum(s * z, 0) * C for z in Z for s in (1, -1)]
def setup_inputs(rng):
    def f(*shape):
        return mx_ref.flush((rng.standard_normal(shape, dtype=np.float32) * np.exp2(rng.integers(-2, 3, shape[:-1] + (1,)))).astype(BF))
    return {"x": f(N, 128, KT * 4 * NC), "w1": f(N, 128, G * KT * 512), "w2": f(N, 128, WT * 512)}
def setup_inputs_blocks(rng):
    d = setup_inputs(rng)
    for k in ("x", "w1", "w2"): d[k] = mx_ref.spread(d[k], rng, 4)
    return d
def setup_inputs_wide(rng):
    d = setup_inputs(rng)
    for k in ("x", "w1", "w2"): d[k] = mx_ref.flush((d[k].astype(np.float32) * np.exp2(rng.integers(-8, 9, (N, 1, 1))).astype(np.float32)).astype(BF))
    return d
def setup_inputs_zeros(rng):
    d = setup_inputs(rng); v = d["x"].reshape(N, 128, -1, 4).copy()
    v[np.broadcast_to((rng.random((N, 1, v.shape[2], 1)) < 0.33), v.shape)] = 0
    d["x"] = v.reshape(d["x"].shape)
    return d
def reference(x, w1, w2):
    H = [mx_ref.quantize(tile(act(layer(w1[j], [mx_ref.quantize(cut(x[j], t, 4 * NC)) for t in range(KT)])))) for j in range(N)]
    y = np.zeros((N, 128, N * WT * NC), np.float32)
    for r in range(N):
        for i in range(WT):
            qw = mx_ref.quantize(cut(w2[r], i))
            for j in range(N):
                y[r][:, NC * (WT * j + i):NC * (WT * j + i) + NC] = mx_ref.matmul(qw, H[j])
    return {"y": y}

@@ -1,0 +1,156 @@
+from concourse.bass import DstId, RemoteDMATransfer
+from concourse.mybir import dt, AluOpType, ActivationFunctionType
+
+NC = 128
+CF = 0.041
+BANK = 512
+
+SCRATCH = {
+    "xb": ("sbuf", [128, 512], "bfloat16"),
+    "w1b": ("sbuf", [128, 1024], "bfloat16"),
+    "w2b": ("sbuf", [128, 512], "bfloat16"),
+    "hb": ("sbuf", [128, 512], "bfloat16"),
+    "xq": ("sbuf", [128, 128], "float8_e4m3fn_x4"),
+    "xs": ("sbuf", [128, 128], "uint8"),
+    "w1q": ("sbuf", [128, 256], "float8_e4m3fn_x4"),
+    "w1s": ("sbuf", [128, 256], "uint8"),
+    "w2q": ("sbuf", [128, 128], "float8_e4m3fn_x4"),
+    "w2s": ("sbuf", [128, 128], "uint8"),
+    "hcod": ("sbuf", [128, 1024], "float8_e4m3fn_x4"),
+    "hsca": ("sbuf", [128, 1024], "uint8"),
+    "ps": ("psum", [128, 8 * BANK], "float32"),
+    "yb": ("sbuf", [128, 1024], "float32"),
+}
+SEMAPHORES = ["ldx", "ldw1", "ldw2", "qx", "qw1a", "qw1b", "qw2", "z0", "z1", "r01", "r23", "qh",
+              "arrk", "arrs", "arrc1", "arrc2", "arrc3", "sent",
+              "m0", "ma1", "ma2", "ma3", "mb1", "mb2", "mb3",
+              "c0", "ca1", "ca2", "ca3", "cb1", "cb2", "cb3", "st"]
+
+
+def _count(mask):
+    return bin(mask).count("1")
+
+
+def rank_program(g, core, T, topo):
+    rank = T.rank_of(core)
+    if rank is None:
+        return
+    S = T.sem
+    ranks = list(T.cores)
+
+    def partner(a):
+        for b in ranks:
+            if (topo.rack(topo.host(b)) != topo.rack(topo.host(a)) and topo.may_write(a, b)
+                    and topo.chip(a) == topo.chip(b)):
+                return b
+
+    def kind(a, b):
+        if topo.host(a) == topo.host(b):
+            return 1
+        return 2 if topo.chip(a) == topo.chip(b) else 3
+
+    peers = sorted([b for b in ranks if topo.same_plane(core, b)], key=lambda b: kind(core, b))
+    mate = partner(core)
+    slot_core = [core, mate]
+    for b in peers:
+        slot_core += [b, partner(b)]
+
+    def codes(a, b):
+        return T.hcod[:, a:b].bitcast(dt.uint8)
+
+    g.sync.dma_start(T.xb[:], T.x[:]).then_inc(S.ldx, 16)
+    g.scalar.dma_start(T.w1b[:], T.w1[:]).then_inc(S.ldw1, 16)
+    g.sync.dma_start(T.w2b[:], T.w2[:]).then_inc(S.ldw2, 16)
+
+    v, te, sc = g.vector, g.tensor, g.scalar
+    v.wait_ge(S.ldx, 16)
+    v.quantize_mx(T.xq[:], T.xs[:], T.xb[:]).then_inc(S.qx, 1)
+    v.wait_ge(S.ldw1, 16)
+    v.quantize_mx(T.w1q[:, 0:128], T.w1s[:, 0:128], T.w1b[:, 0:512]).then_inc(S.qw1a, 1)
+    v.quantize_mx(T.w1q[:, 128:256], T.w1s[:, 128:256], T.w1b[:, 512:1024]).then_inc(S.qw1b, 1)
+
+    te.wait_ge(S.qx, 1)
+    te.wait_ge(S.qw1a, 1)
+    te.matmul_mx(T.ps[:, 0:NC], T.w1q[:, 0:128], T.w1s[:, 0:128], T.xq[:], T.xs[:], True, True).then_inc(S.z0, 1)
+    te.wait_ge(S.qw1b, 1)
+    te.matmul_mx(T.ps[:, BANK:BANK + NC], T.w1q[:, 128:256], T.w1s[:, 128:256], T.xq[:], T.xs[:], True, True).then_inc(S.z1, 1)
+
+    v.wait_ge(S.z0, 1)
+    v.tensor_scalar(T.hb[:, 0:512:4], T.ps[:, 0:NC], 0.0, CF, AluOpType.max, AluOpType.mult).then_inc(S.r01, 1)
+    v.tensor_scalar(T.hb[:, 1:512:4], T.ps[:, 0:NC], -CF, 0.0, AluOpType.mult, AluOpType.max).then_inc(S.r01, 1)
+    sc.wait_ge(S.z1, 1)
+    sc.activation(T.hb[:, 2:512:4], T.ps[:, BANK:BANK + NC], ActivationFunctionType.Relu, scale=CF).then_inc(S.r23, 1)
+    sc.activation(T.hb[:, 3:512:4], T.ps[:, BANK:BANK + NC], ActivationFunctionType.Relu, scale=-CF).then_inc(S.r23, 1)
+    v.wait_ge(S.r01, 2)
+    v.wait_ge(S.r23, 2)
+    v.quantize_mx(T.hcod[:, 0:NC], T.hsca[:, 0:NC], T.hb[:]).then_inc(S.qh, 1)
+    v.wait_ge(S.ldw2, 16)
+    v.quantize_mx(T.w2q[:], T.w2s[:], T.w2b[:]).then_inc(S.qw2, 1)
+
+    sent = 0
+    g.wait_ge(S.qh, 1)
+    rid, pid = topo.addr(mate, core)
+    mk = topo.mask(core, mate)
+    g.remote_dma(T.hsca[:, NC:2 * NC], T.hsca[:, 0:NC], S.arrk, S.sent, pid, rid, mk)
+    g.remote_dma(codes(NC, 2 * NC), codes(0, NC), S.arrk, S.sent, pid, rid, mk)
+    sent += 2 * _count(mk)
+    n_k = 2 * _count(topo.mask(mate, core))
+
+    g.wait_ge(S.arrk, n_k)
+    mp = topo.mask(core, peers[0])
+    for b in peers:
+        mp &= topo.mask(core, b)
+    ids, dsts = [], []
+    for b in peers:
+        rid, pid = topo.addr(b, core)
+        k = kind(core, b)
+        ids.append(DstId(rid=rid, pnc=pid))
+        dsts.append(T.hsca[:, 2 * NC * k:2 * NC * (k + 1)])
+    g.remote_dma_fused([RemoteDMATransfer(dst_ids=ids, dma_engine_mask=mp, remote_sem=S.arrs,
+                                          srcs=[T.hsca[:, 0:2 * NC]], dsts=dsts)], local_sem=S.sent)
+    sent += _count(mp)
+    for b in peers:
+        rid, pid = topo.addr(b, core)
+        k = kind(core, b)
+        g.remote_dma(codes(2 * NC * k, 2 * NC * (k + 1)), codes(0, 2 * NC), S["arrc%d" % k], S.sent, pid, rid, mp)
+        sent += _count(mp)
+
+    def mm(bank, a, b):
+        return te.matmul_mx(T.ps[:, bank * BANK:bank * BANK + (b - a)], T.w2q[:], T.w2s[:],
+                            T.hcod[:, a:b], T.hsca[:, a:b], True, True)
+
+    def store(q, s):
+        r = T.rank_of(slot_core[s])
+        return q.dma_start(T.y[:, NC * r:NC * (r + 1)], T.yb[:, NC * s:NC * (s + 1)]).then_inc(S.st, 16)
+
+    te.wait_ge(S.qh, 1)
+    te.wait_ge(S.qw2, 1)
+    te.wait_ge(S.arrk, n_k)
+    mm(0, 0, 2 * NC).then_inc(S.m0, 1)
+    v.wait_ge(S.m0, 1)
+    v.tensor_copy(T.yb[:, 0:2 * NC], T.ps[:, 0:2 * NC]).then_inc(S.c0, 1)
+    g.sync.wait_ge(S.c0, 1)
+    store(g.sync, 0)
+    store(g.sync, 1)
+    stores = 2
+
+    te.wait_ge(S.arrs, sum(_count(topo.mask(b, core)) for b in peers))
+    for b in peers:
+        k = kind(core, b)
+        sa, sb = 2 * k, 2 * k + 1
+        te.wait_ge(S["arrc%d" % k], _count(topo.mask(b, core)))
+        mm(sa, NC * sa, NC * (sa + 1)).then_inc(S["ma%d" % k], 1)
+        mm(sb, NC * sb, NC * (sb + 1)).then_inc(S["mb%d" % k], 1)
+        v.wait_ge(S["ma%d" % k], 1)
+        v.tensor_copy(T.yb[:, NC * sa:NC * (sa + 1)], T.ps[:, sa * BANK:sa * BANK + NC]).then_inc(S["ca%d" % k], 1)
+        g.sync.wait_ge(S["ca%d" % k], 1)
+        store(g.sync, sa)
+        sc.wait_ge(S["mb%d" % k], 1)
+        sc.activation(T.yb[:, NC * sb:NC * (sb + 1)], T.ps[:, sb * BANK:sb * BANK + NC],
+                      ActivationFunctionType.Copy).then_inc(S["cb%d" % k], 1)
+        sc.wait_ge(S["cb%d" % k], 1)
+        store(sc, sb)
+        stores += 2
+
+    g.wait_ge(S.sent, sent)
+    g.sync.wait_ge(S.st, 16 * stores)

@@ -22,7 +22,7 @@ SCRATCH = {
     "yb": ("sbuf", [128, 1024], "float32"),
 }
 SEMAPHORES = ["ldx", "ldw1", "ldw2", "qx", "qw1a", "qw1b", "qw2", "z0", "z1", "r01", "r23", "qh",
-              "arrk", "arrs", "arrc1", "arrc2", "arrc3", "sent",
+              "arrks", "arrkc", "arrs", "arrc1", "arrc2", "arrc3", "sent",
               "m0", "ma1", "ma2", "ma3", "mb1", "mb2", "mb3",
               "c0", "ca1", "ca2", "ca3", "cb1", "cb2", "cb3", "st"]
 
@@ -51,18 +51,21 @@ def rank_program(g, core, T, topo):
 
     peers = sorted([b for b in ranks if topo.same_plane(core, b)], key=lambda b: kind(core, b))
     mate = partner(core)
-    slot_core = [core, mate]
+    slot_rank = [rank, T.rank_of(mate)]
     for b in peers:
-        slot_core += [b, partner(b)]
+        slot_rank += [T.rank_of(b), T.rank_of(partner(b))]
 
     def codes(a, b):
         return T.hcod[:, a:b].bitcast(dt.uint8)
 
-    g.sync.dma_start(T.xb[:], T.x[:]).then_inc(S.ldx, 16)
-    g.scalar.dma_start(T.w1b[:], T.w1[:]).then_inc(S.ldw1, 16)
-    g.sync.dma_start(T.w2b[:], T.w2[:]).then_inc(S.ldw2, 16)
+    v, te, sc, sy = g.vector, g.tensor, g.scalar, g.sync
 
-    v, te, sc = g.vector, g.tensor, g.scalar
+    sy.dma_start(T.xb[:], T.x[:]).then_inc(S.ldx, 16)
+    sc.dma_start(T.w1b[:], T.w1[:]).then_inc(S.ldw1, 16)
+    sy.wait_ge(S.ldx, 16)
+    sy.wait_ge(S.ldw1, 16)
+    sy.dma_start(T.w2b[:], T.w2[:]).then_inc(S.ldw2, 16)
+
     v.wait_ge(S.ldx, 16)
     v.quantize_mx(T.xq[:], T.xs[:], T.xb[:]).then_inc(S.qx, 1)
     v.wait_ge(S.ldw1, 16)
@@ -91,12 +94,11 @@ def rank_program(g, core, T, topo):
     g.wait_ge(S.qh, 1)
     rid, pid = topo.addr(mate, core)
     mk = topo.mask(core, mate)
-    g.remote_dma(T.hsca[:, NC:2 * NC], T.hsca[:, 0:NC], S.arrk, S.sent, pid, rid, mk)
-    g.remote_dma(codes(NC, 2 * NC), codes(0, NC), S.arrk, S.sent, pid, rid, mk)
+    g.remote_dma(T.hsca[:, NC:2 * NC], T.hsca[:, 0:NC], S.arrks, S.sent, pid, rid, mk)
+    g.remote_dma(codes(NC, 2 * NC), codes(0, NC), S.arrkc, S.sent, pid, rid, mk)
     sent += 2 * _count(mk)
-    n_k = 2 * _count(topo.mask(mate, core))
+    n_k = _count(topo.mask(mate, core))
 
-    g.wait_ge(S.arrk, n_k)
     mp = topo.mask(core, peers[0])
     for b in peers:
         mp &= topo.mask(core, b)
@@ -106,9 +108,11 @@ def rank_program(g, core, T, topo):
         k = kind(core, b)
         ids.append(DstId(rid=rid, pnc=pid))
         dsts.append(T.hsca[:, 2 * NC * k:2 * NC * (k + 1)])
+    g.wait_ge(S.arrks, n_k)
     g.remote_dma_fused([RemoteDMATransfer(dst_ids=ids, dma_engine_mask=mp, remote_sem=S.arrs,
                                           srcs=[T.hsca[:, 0:2 * NC]], dsts=dsts)], local_sem=S.sent)
     sent += _count(mp)
+    g.wait_ge(S.arrkc, n_k)
     for b in peers:
         rid, pid = topo.addr(b, core)
         k = kind(core, b)
@@ -119,20 +123,33 @@ def rank_program(g, core, T, topo):
         return te.matmul_mx(T.ps[:, bank * BANK:bank * BANK + (b - a)], T.w2q[:], T.w2s[:],
                             T.hcod[:, a:b], T.hsca[:, a:b], True, True)
 
-    def store(q, s):
-        r = T.rank_of(slot_core[s])
-        return q.dma_start(T.y[:, NC * r:NC * (r + 1)], T.yb[:, NC * s:NC * (s + 1)]).then_inc(S.st, 16)
+    def yblk(s):
+        return slice(NC * slot_rank[s], NC * (slot_rank[s] + 1))
+
+    stores = [0]
+
+    def store(q, slots):
+        rs = sorted(slot_rank[s] for s in slots)
+        runs = []
+        for r in rs:
+            if runs and runs[-1][1] == r:
+                runs[-1][1] = r + 1
+            else:
+                runs.append([r, r + 1])
+        for a, b in runs:
+            q.dma_start(T.y[:, NC * a:NC * b], T.yb[:, NC * a:NC * b]).then_inc(S.st, 16)
+            stores[0] += 1
 
     te.wait_ge(S.qh, 1)
     te.wait_ge(S.qw2, 1)
-    te.wait_ge(S.arrk, n_k)
+    te.wait_ge(S.arrks, n_k)
+    te.wait_ge(S.arrkc, n_k)
     mm(0, 0, 2 * NC).then_inc(S.m0, 1)
     v.wait_ge(S.m0, 1)
-    v.tensor_copy(T.yb[:, 0:2 * NC], T.ps[:, 0:2 * NC]).then_inc(S.c0, 1)
-    g.sync.wait_ge(S.c0, 1)
-    store(g.sync, 0)
-    store(g.sync, 1)
-    stores = 2
+    v.tensor_copy(T.yb[:, yblk(0)], T.ps[:, 0:NC]).then_inc(S.c0, 1)
+    v.tensor_copy(T.yb[:, yblk(1)], T.ps[:, NC:2 * NC]).then_inc(S.c0, 1)
+    sy.wait_ge(S.c0, 2)
+    sc.wait_ge(S.c0, 2)
 
     te.wait_ge(S.arrs, sum(_count(topo.mask(b, core)) for b in peers))
     for b in peers:
@@ -142,15 +159,14 @@ def rank_program(g, core, T, topo):
         mm(sa, NC * sa, NC * (sa + 1)).then_inc(S["ma%d" % k], 1)
         mm(sb, NC * sb, NC * (sb + 1)).then_inc(S["mb%d" % k], 1)
         v.wait_ge(S["ma%d" % k], 1)
-        v.tensor_copy(T.yb[:, NC * sa:NC * (sa + 1)], T.ps[:, sa * BANK:sa * BANK + NC]).then_inc(S["ca%d" % k], 1)
-        g.sync.wait_ge(S["ca%d" % k], 1)
-        store(g.sync, sa)
+        v.tensor_copy(T.yb[:, yblk(sa)], T.ps[:, sa * BANK:sa * BANK + NC]).then_inc(S["ca%d" % k], 1)
+        sy.wait_ge(S["ca%d" % k], 1)
+        store(sy, [0, sa] if k == 1 else [sa])
         sc.wait_ge(S["mb%d" % k], 1)
-        sc.activation(T.yb[:, NC * sb:NC * (sb + 1)], T.ps[:, sb * BANK:sb * BANK + NC],
+        sc.activation(T.yb[:, yblk(sb)], T.ps[:, sb * BANK:sb * BANK + NC],
                       ActivationFunctionType.Copy).then_inc(S["cb%d" % k], 1)
         sc.wait_ge(S["cb%d" % k], 1)
-        store(sc, sb)
-        stores += 2
+        store(sc, [1, sb] if k == 1 else [sb])
 
     g.wait_ge(S.sent, sent)
-    g.sync.wait_ge(S.st, 16 * stores)
+    sy.wait_ge(S.st, 16 * stores[0])

@@ -4,6 +4,7 @@ from concourse.mybir import dt, AluOpType, ActivationFunctionType
 NC = 128
 CF = 0.041
 BANK = 512
+WORLD = 512
 
 SCRATCH = {
     "xb": ("sbuf", [128, 512], "bfloat16"),
@@ -22,7 +23,7 @@ SCRATCH = {
     "yb": ("sbuf", [128, 1024], "float32"),
 }
 SEMAPHORES = ["ldx", "ldw1", "ldw2", "qx", "qw1a", "qw1b", "qw2", "z0", "z1", "r01", "r23", "qh",
-              "arrks", "arrkc", "arrs", "arrc1", "arrc2", "arrc3", "sent",
+              "arrks", "arrkc", "arrs", "hco", "arro1", "arro2", "arro3", "arrc1", "arrc2", "arrc3", "sent",
               "m0", "ma1", "ma2", "ma3", "mb1", "mb2", "mb3",
               "c0", "ca1", "ca2", "ca3", "cb1", "cb2", "cb3", "st"]
 
@@ -33,10 +34,11 @@ def _count(mask):
 
 def rank_program(g, core, T, topo):
     rank = T.rank_of(core)
-    if rank is None:
-        return
     S = T.sem
     ranks = list(T.cores)
+
+    def same_chip(a, b):
+        return topo.host(a) == topo.host(b) and topo.chip(a) == topo.chip(b)
 
     def partner(a):
         for b in ranks:
@@ -49,14 +51,44 @@ def rank_program(g, core, T, topo):
             return 1
         return 2 if topo.chip(a) == topo.chip(b) else 3
 
-    peers = sorted([b for b in ranks if topo.same_plane(core, b)], key=lambda b: kind(core, b))
-    mate = partner(core)
-    slot_rank = [rank, T.rank_of(mate)]
-    for b in peers:
-        slot_rank += [T.rank_of(b), T.rank_of(partner(b))]
+    def peers_of(a):
+        return sorted([b for b in ranks if topo.same_plane(a, b)], key=lambda b: kind(a, b))
+
+    def helper(a):
+        for c in range(WORLD):
+            if same_chip(a, c) and topo.die(c) != topo.die(a):
+                return c
+
+    def chip_only(a):
+        return topo.mask(a, helper(a)) & ~topo.mask(a, partner(a))
 
     def codes(a, b):
         return T.hcod[:, a:b].bitcast(dt.uint8)
+
+    if rank is None:
+        owner = None
+        for a in ranks:
+            if same_chip(a, core) and helper(a) == core:
+                owner = a
+        if owner is None:
+            return
+        g.wait_ge(S.hco, _count(chip_only(owner)))
+        sent = 0
+        for b in peers_of(owner)[1:]:
+            k = kind(owner, b)
+            rid, pid = topo.addr(b, core)
+            mk = topo.mask(core, b)
+            g.remote_dma(codes(2 * NC * k, 2 * NC * k + NC), codes(0, NC), S["arro%d" % k], S.sent, pid, rid, mk)
+            sent += _count(mk)
+        g.wait_ge(S.sent, sent)
+        return
+
+    peers = peers_of(core)
+    mate = partner(core)
+    aide = helper(core)
+    slot_rank = [rank, T.rank_of(mate)]
+    for b in peers:
+        slot_rank += [T.rank_of(b), T.rank_of(partner(b))]
 
     v, te, sc, sy = g.vector, g.tensor, g.scalar, g.sync
 
@@ -102,6 +134,15 @@ def rank_program(g, core, T, topo):
     mp = topo.mask(core, peers[0])
     for b in peers:
         mp &= topo.mask(core, b)
+    rid, pid = topo.addr(aide, core)
+    mh = chip_only(core)
+    g.remote_dma(codes(0, NC), codes(0, NC), S.hco, S.sent, pid, rid, mh)
+    sent += _count(mh)
+    rid, pid = topo.addr(peers[0], core)
+    k = kind(core, peers[0])
+    g.remote_dma(codes(2 * NC * k, 2 * NC * k + NC), codes(0, NC), S["arro%d" % k], S.sent, pid, rid, mp)
+    sent += _count(mp)
+
     ids, dsts = [], []
     for b in peers:
         rid, pid = topo.addr(b, core)
@@ -116,7 +157,7 @@ def rank_program(g, core, T, topo):
     for b in peers:
         rid, pid = topo.addr(b, core)
         k = kind(core, b)
-        g.remote_dma(codes(2 * NC * k, 2 * NC * (k + 1)), codes(0, 2 * NC), S["arrc%d" % k], S.sent, pid, rid, mp)
+        g.remote_dma(codes(2 * NC * k + NC, 2 * NC * (k + 1)), codes(NC, 2 * NC), S["arrc%d" % k], S.sent, pid, rid, mp)
         sent += _count(mp)
 
     def mm(bank, a, b):
@@ -152,16 +193,34 @@ def rank_program(g, core, T, topo):
     sc.wait_ge(S.c0, 2)
 
     te.wait_ge(S.arrs, sum(_count(topo.mask(b, core)) for b in peers))
-    for b in peers:
-        k = kind(core, b)
-        sa, sb = 2 * k, 2 * k + 1
+
+    def own_block(k):
+        b = peers[k - 1]
+        src = b if k == 1 else helper(b)
+        te.wait_ge(S["arro%d" % k], _count(topo.mask(src, core)))
+        mm(2 * k, NC * 2 * k, NC * (2 * k + 1)).then_inc(S["ma%d" % k], 1)
+
+    def passed_block(k):
+        b = peers[k - 1]
         te.wait_ge(S["arrc%d" % k], _count(topo.mask(b, core)))
-        mm(sa, NC * sa, NC * (sa + 1)).then_inc(S["ma%d" % k], 1)
-        mm(sb, NC * sb, NC * (sb + 1)).then_inc(S["mb%d" % k], 1)
+        mm(2 * k + 1, NC * (2 * k + 1), NC * (2 * k + 2)).then_inc(S["mb%d" % k], 1)
+
+    own_block(1)
+    own_block(2)
+    passed_block(1)
+    own_block(3)
+    passed_block(2)
+    passed_block(3)
+
+    for k in (1, 2, 3):
+        sa, sb = 2 * k, 2 * k + 1
         v.wait_ge(S["ma%d" % k], 1)
         v.tensor_copy(T.yb[:, yblk(sa)], T.ps[:, sa * BANK:sa * BANK + NC]).then_inc(S["ca%d" % k], 1)
         sy.wait_ge(S["ca%d" % k], 1)
-        store(sy, [0, sa] if k == 1 else [sa])
+        if k == 1:
+            store(sy, [0, sa])
+        elif k == 3:
+            store(sy, [sa - 2, sa])
         sc.wait_ge(S["mb%d" % k], 1)
         sc.activation(T.yb[:, yblk(sb)], T.ps[:, sb * BANK:sb * BANK + NC],
                       ActivationFunctionType.Copy).then_inc(S["cb%d" % k], 1)

from concourse.bass import DstId, RemoteDMATransfer
from concourse.mybir import dt, AluOpType, ActivationFunctionType

NC = 128
CF = 0.041
BANK = 512
WORLD = 512

SCRATCH = {
    "xb": ("sbuf", [128, 512], "bfloat16"),
    "w1b": ("sbuf", [128, 1024], "bfloat16"),
    "w2b": ("sbuf", [128, 512], "bfloat16"),
    "hb": ("sbuf", [128, 512], "bfloat16"),
    "xq": ("sbuf", [128, 128], "float8_e4m3fn_x4"),
    "xs": ("sbuf", [128, 128], "uint8"),
    "w1q": ("sbuf", [128, 256], "float8_e4m3fn_x4"),
    "w1s": ("sbuf", [128, 256], "uint8"),
    "w2q": ("sbuf", [128, 128], "float8_e4m3fn_x4"),
    "w2s": ("sbuf", [128, 128], "uint8"),
    "hcod": ("sbuf", [128, 1024], "float8_e4m3fn_x4"),
    "hsca": ("sbuf", [128, 1024], "uint8"),
    "ps": ("psum", [128, 8 * BANK], "float32"),
    "yb": ("sbuf", [128, 1024], "float32"),
}
SEMAPHORES = ["ldx", "ldw1", "ldw2", "qx", "qw1a", "qw1b", "qw2", "z0", "z1", "r01", "r23", "qh",
              "arrks", "arrkc", "arrs", "hco", "arro1", "arro2", "arro3", "arrc1", "arrc2", "arrc3", "sent",
              "m0", "ma1", "ma2", "ma3", "mb1", "mb2", "mb3",
              "c0", "ca1", "ca2", "ca3", "cb1", "cb2", "cb3", "st"]


def _count(mask):
    return bin(mask).count("1")


def rank_program(g, core, T, topo):
    rank = T.rank_of(core)
    S = T.sem
    ranks = list(T.cores)

    def same_chip(a, b):
        return topo.host(a) == topo.host(b) and topo.chip(a) == topo.chip(b)

    def partner(a):
        for b in ranks:
            if (topo.rack(topo.host(b)) != topo.rack(topo.host(a)) and topo.may_write(a, b)
                    and topo.chip(a) == topo.chip(b)):
                return b

    def kind(a, b):
        if topo.host(a) == topo.host(b):
            return 1
        return 2 if topo.chip(a) == topo.chip(b) else 3

    def peers_of(a):
        return sorted([b for b in ranks if topo.same_plane(a, b)], key=lambda b: kind(a, b))

    def helper(a):
        for c in range(WORLD):
            if same_chip(a, c) and topo.die(c) != topo.die(a):
                return c

    def chip_only(a):
        return topo.mask(a, helper(a)) & ~topo.mask(a, partner(a))

    def codes(a, b):
        return T.hcod[:, a:b].bitcast(dt.uint8)

    if rank is None:
        owner = None
        for a in ranks:
            if same_chip(a, core) and helper(a) == core:
                owner = a
        if owner is None:
            return
        g.wait_ge(S.hco, _count(chip_only(owner)))
        sent = 0
        for b in peers_of(owner)[1:]:
            k = kind(owner, b)
            rid, pid = topo.addr(b, core)
            mk = topo.mask(core, b)
            g.remote_dma(codes(2 * NC * k, 2 * NC * k + NC), codes(0, NC), S["arro%d" % k], S.sent, pid, rid, mk)
            sent += _count(mk)
        g.wait_ge(S.sent, sent)
        return

    peers = peers_of(core)
    mate = partner(core)
    aide = helper(core)
    slot_rank = [rank, T.rank_of(mate)]
    for b in peers:
        slot_rank += [T.rank_of(b), T.rank_of(partner(b))]

    v, te, sc, sy = g.vector, g.tensor, g.scalar, g.sync

    sy.dma_start(T.xb[:], T.x[:]).then_inc(S.ldx, 16)
    sc.dma_start(T.w1b[:], T.w1[:]).then_inc(S.ldw1, 16)
    sy.wait_ge(S.ldx, 16)
    sy.wait_ge(S.ldw1, 16)
    sy.dma_start(T.w2b[:], T.w2[:]).then_inc(S.ldw2, 16)

    v.wait_ge(S.ldx, 16)
    v.quantize_mx(T.xq[:], T.xs[:], T.xb[:]).then_inc(S.qx, 1)
    v.wait_ge(S.ldw1, 16)
    v.quantize_mx(T.w1q[:, 0:128], T.w1s[:, 0:128], T.w1b[:, 0:512]).then_inc(S.qw1a, 1)
    v.quantize_mx(T.w1q[:, 128:256], T.w1s[:, 128:256], T.w1b[:, 512:1024]).then_inc(S.qw1b, 1)

    te.wait_ge(S.qx, 1)
    te.wait_ge(S.qw1a, 1)
    te.matmul_mx(T.ps[:, 0:NC], T.w1q[:, 0:128], T.w1s[:, 0:128], T.xq[:], T.xs[:], True, True).then_inc(S.z0, 1)
    te.wait_ge(S.qw1b, 1)
    te.matmul_mx(T.ps[:, BANK:BANK + NC], T.w1q[:, 128:256], T.w1s[:, 128:256], T.xq[:], T.xs[:], True, True).then_inc(S.z1, 1)

    v.wait_ge(S.z0, 1)
    v.tensor_scalar(T.hb[:, 0:512:4], T.ps[:, 0:NC], 0.0, CF, AluOpType.max, AluOpType.mult).then_inc(S.r01, 1)
    v.tensor_scalar(T.hb[:, 1:512:4], T.ps[:, 0:NC], -CF, 0.0, AluOpType.mult, AluOpType.max).then_inc(S.r01, 1)
    sc.wait_ge(S.z1, 1)
    sc.activation(T.hb[:, 2:512:4], T.ps[:, BANK:BANK + NC], ActivationFunctionType.Relu, scale=CF).then_inc(S.r23, 1)
    sc.activation(T.hb[:, 3:512:4], T.ps[:, BANK:BANK + NC], ActivationFunctionType.Relu, scale=-CF).then_inc(S.r23, 1)
    v.wait_ge(S.r01, 2)
    v.wait_ge(S.r23, 2)
    v.quantize_mx(T.hcod[:, 0:NC], T.hsca[:, 0:NC], T.hb[:]).then_inc(S.qh, 1)
    v.wait_ge(S.ldw2, 16)
    v.quantize_mx(T.w2q[:], T.w2s[:], T.w2b[:]).then_inc(S.qw2, 1)

    sent = 0
    g.wait_ge(S.qh, 1)
    rid, pid = topo.addr(mate, core)
    mk = topo.mask(core, mate)
    g.remote_dma(T.hsca[:, NC:2 * NC], T.hsca[:, 0:NC], S.arrks, S.sent, pid, rid, mk)
    g.remote_dma(codes(NC, 2 * NC), codes(0, NC), S.arrkc, S.sent, pid, rid, mk)
    sent += 2 * _count(mk)
    n_k = _count(topo.mask(mate, core))

    mp = topo.mask(core, peers[0])
    for b in peers:
        mp &= topo.mask(core, b)
    rid, pid = topo.addr(aide, core)
    mh = chip_only(core)
    g.remote_dma(codes(0, NC), codes(0, NC), S.hco, S.sent, pid, rid, mh)
    sent += _count(mh)
    rid, pid = topo.addr(peers[0], core)
    k = kind(core, peers[0])
    g.remote_dma(codes(2 * NC * k, 2 * NC * k + NC), codes(0, NC), S["arro%d" % k], S.sent, pid, rid, mp)
    sent += _count(mp)

    ids, dsts = [], []
    for b in peers:
        rid, pid = topo.addr(b, core)
        k = kind(core, b)
        ids.append(DstId(rid=rid, pnc=pid))
        dsts.append(T.hsca[:, 2 * NC * k:2 * NC * (k + 1)])
    g.wait_ge(S.arrks, n_k)
    g.remote_dma_fused([RemoteDMATransfer(dst_ids=ids, dma_engine_mask=mp, remote_sem=S.arrs,
                                          srcs=[T.hsca[:, 0:2 * NC]], dsts=dsts)], local_sem=S.sent)
    sent += _count(mp)
    g.wait_ge(S.arrkc, n_k)
    for b in peers:
        rid, pid = topo.addr(b, core)
        k = kind(core, b)
        g.remote_dma(codes(2 * NC * k + NC, 2 * NC * (k + 1)), codes(NC, 2 * NC), S["arrc%d" % k], S.sent, pid, rid, mp)
        sent += _count(mp)

    def mm(bank, a, b):
        return te.matmul_mx(T.ps[:, bank * BANK:bank * BANK + (b - a)], T.w2q[:], T.w2s[:],
                            T.hcod[:, a:b], T.hsca[:, a:b], True, True)

    def yblk(s):
        return slice(NC * slot_rank[s], NC * (slot_rank[s] + 1))

    stores = [0]

    def store(q, slots):
        rs = sorted(slot_rank[s] for s in slots)
        runs = []
        for r in rs:
            if runs and runs[-1][1] == r:
                runs[-1][1] = r + 1
            else:
                runs.append([r, r + 1])
        for a, b in runs:
            q.dma_start(T.y[:, NC * a:NC * b], T.yb[:, NC * a:NC * b]).then_inc(S.st, 16)
            stores[0] += 1

    te.wait_ge(S.qh, 1)
    te.wait_ge(S.qw2, 1)
    te.wait_ge(S.arrks, n_k)
    te.wait_ge(S.arrkc, n_k)
    mm(0, 0, 2 * NC).then_inc(S.m0, 1)
    v.wait_ge(S.m0, 1)
    v.tensor_copy(T.yb[:, yblk(0)], T.ps[:, 0:NC]).then_inc(S.c0, 1)
    v.tensor_copy(T.yb[:, yblk(1)], T.ps[:, NC:2 * NC]).then_inc(S.c0, 1)
    sy.wait_ge(S.c0, 2)
    sc.wait_ge(S.c0, 2)

    te.wait_ge(S.arrs, sum(_count(topo.mask(b, core)) for b in peers))

    def own_block(k):
        b = peers[k - 1]
        src = b if k == 1 else helper(b)
        te.wait_ge(S["arro%d" % k], _count(topo.mask(src, core)))
        mm(2 * k, NC * 2 * k, NC * (2 * k + 1)).then_inc(S["ma%d" % k], 1)

    def passed_block(k):
        b = peers[k - 1]
        te.wait_ge(S["arrc%d" % k], _count(topo.mask(b, core)))
        mm(2 * k + 1, NC * (2 * k + 1), NC * (2 * k + 2)).then_inc(S["mb%d" % k], 1)

    own_block(1)
    own_block(2)
    passed_block(1)
    own_block(3)
    passed_block(2)
    passed_block(3)

    for k in (1, 2, 3):
        sa, sb = 2 * k, 2 * k + 1
        v.wait_ge(S["ma%d" % k], 1)
        v.tensor_copy(T.yb[:, yblk(sa)], T.ps[:, sa * BANK:sa * BANK + NC]).then_inc(S["ca%d" % k], 1)
        sy.wait_ge(S["ca%d" % k], 1)
        if k == 1:
            store(sy, [0, sa])
        elif k == 3:
            store(sy, [sa - 2, sa])
        sc.wait_ge(S["mb%d" % k], 1)
        sc.activation(T.yb[:, yblk(sb)], T.ps[:, sb * BANK:sb * BANK + NC],
                      ActivationFunctionType.Copy).then_inc(S["cb%d" % k], 1)
        sc.wait_ge(S["cb%d" % k], 1)
        store(sc, [1, sb] if k == 1 else [sb])

    g.wait_ge(S.sent, sent)
    sy.wait_ge(S.st, 16 * stores[0])
